import numpy as np
import ml_dtypes


def mxq(x, axis, fmt="e4m3"):
    dtype, down = {"e4m3": (ml_dtypes.float8_e4m3fn, 7), "e5m2": (ml_dtypes.float8_e5m2, 14)}[fmt]
    v = np.moveaxis(np.asarray(x, np.float32).astype(ml_dtypes.bfloat16).astype(np.float64), axis, -1)
    blocks = v.reshape(v.shape[:-1] + (-1, 32))
    amax = np.abs(blocks).max(-1, keepdims=True)
    byte = np.maximum(np.where(amax > 0, np.frexp(amax)[1] - 1 + 127, 0) - down, 1)
    scale = np.exp2(byte - 127.0)
    codes = (blocks / scale).astype(np.float32).astype(dtype).astype(np.float64)
    return np.moveaxis((codes * scale).reshape(v.shape), -1, axis)


WIDE = False


def mx_kscale(k):
    if not WIDE:
        return np.ones(k)
    levels = np.array([10, -10, 5, -5, 0])
    if k % 512:
        return np.exp2(np.random.permutation(np.resize(levels, k // 32))).repeat(32)
    a = np.empty((k // 512, 16))
    for p in range(k // 512):
        a[p, :8] = np.random.permutation(np.resize(levels, 8))
        for g in range(8):
            far = levels[np.abs(levels - a[p, g]) >= 10]
            a[p, g + 8] = far[np.random.randint(len(far))]
    return np.exp2(a.ravel()).repeat(32)


def f64(x):
    return np.asarray(x).astype(np.float64)


def striped(idx):
    return np.tile(idx.reshape(-1, 16).T, (8, 1)).astype(np.uint16)


def unstriped(offs):
    return offs[:16].T.reshape(-1).astype(np.int64)


def pack_weight(w):
    k, n = w.shape
    w = f64(np.asarray(w, np.float32).astype(ml_dtypes.bfloat16)).reshape(k // 32, 32, n)
    amax = np.abs(w).max(1)
    byte = np.clip(np.where(amax > 0, np.frexp(amax)[1] - 1 + 127 - 7, 1), 1, 254)
    scaled = (w * np.exp2(127.0 - byte)[:, None, :]).reshape(k, n).astype(np.float32)
    words = np.ascontiguousarray(scaled.reshape(k // 512, 128, 4, n).transpose(0, 1, 3, 2)).astype(ml_dtypes.float8_e4m3fn).view(np.uint8)
    return words, np.ascontiguousarray(byte.astype(np.uint8).reshape(k // 512, 16, n))


def unpack_weight(words, scales):
    g, p, n, _ = words.shape
    vals = np.ascontiguousarray(words).view(ml_dtypes.float8_e4m3fn).astype(np.float64) * np.repeat(np.exp2(scales.astype(np.float64) - 127.0), 8, axis=1)[..., None]
    return vals.transpose(0, 1, 3, 2).reshape(g * 512, n)


def sigmoid(v):
    return 1.0 / (1.0 + np.exp(-np.maximum(v, -700.0)))


K, T, S, J = 1024, 2048, 512, 256


def setup_inputs():
    n = np.random.standard_normal
    s = mx_kscale(K)[:, None]
    packed_xT = pack_weight(n((K, T)) * s)
    return {
        "x_words": packed_xT[0],
        "x_scales": packed_xT[1],
        "hT": (n((K, J)) / np.sqrt(K) / s).astype(np.float32),
        "offs": striped(np.random.permutation(T)[:S]),
    }


def reference(x_words, x_scales, hT, offs):
    hTq = mxq(f64(hT), 0, "e4m3")
    xq = unpack_weight(x_words, x_scales)[:, unstriped(offs)]
    y = hTq.T @ xq
    p = sigmoid(y)
    out = np.zeros((J, T))
    out[:, unstriped(offs)] = p
    return out

@@ -1,0 +1,101 @@
+from contextlib import ExitStack
+
+import concourse.mybir as mybir
+
+K, T, S, J = 1024, 2048, 512, 256
+FLOPS = 2 * K * S * J
+
+F32 = mybir.dt.float32
+BF16 = mybir.dt.bfloat16
+I32 = mybir.dt.int32
+U32 = mybir.dt.uint32
+U16 = mybir.dt.uint16
+U8 = mybir.dt.uint8
+FP8X4 = mybir.dt.float8_e4m3fn_x4
+SIGMOID = mybir.ActivationFunctionType.Sigmoid
+
+P = 128
+PACK = 4
+PASSES = K // (P * PACK)
+HALF = S // 2
+
+
+def tile_picked_zvoc_sigmoid_p_kernel(tc, x_words, x_scales, hT, offs, out):
+    nc = tc.nc
+    with ExitStack() as ctx:
+        keep = ctx.enter_context(tc.tile_pool(name="keep", bufs=1))
+        psum = ctx.enter_context(tc.psum_pool(name="psum", bufs=1))
+
+        offsets = keep.tile([P, S // 16], U16, name="offsets")
+        scale_table = keep.tile([P, T], U8, name="scale_table", align_bytes=64)
+        scale_picked = keep.tile([P, S], U8, name="scale_picked", align_bytes=64)
+        x_planes = keep.tile([P, PASSES * S], U8, name="x_planes", align_bytes=64)
+        h_raw = [keep.tile([P, PACK, J], F32, name="h_raw%d" % o, align_bytes=64) for o in range(PASSES)]
+        h_grouped = [keep.tile([P, J, PACK], BF16, name="h_grouped%d" % o, align_bytes=64) for o in range(PASSES)]
+        h_codes = [keep.tile([P, J], U32, name="h_codes%d" % o, align_bytes=64) for o in range(PASSES)]
+        h_planes = [keep.tile([P, J], U8, name="h_planes%d" % o, align_bytes=64) for o in range(PASSES)]
+        word_table = [keep.tile([P, T], U32, name="word_table%d" % o, align_bytes=64) for o in range(PASSES)]
+        x_codes = [keep.tile([P, S], U32, name="x_codes%d" % o, align_bytes=64) for o in range(PASSES)]
+        window = [keep.tile([P, T], F32, name="window%d" % t, align_bytes=64) for t in range(J // P)]
+        probs = [keep.tile([P, S], F32, name="probs%d" % t, align_bytes=64) for t in range(J // P)]
+
+        nc.vector.memset(scale_table[:].bitcast(I32), 0)
+        nc.vector.memset(x_planes[:].bitcast(I32), 0)
+
+        nc.sync.dma_start(offsets[:], offs)
+        nc.sync.dma_start(h_raw[0][:], hT[0:512, :].rearrange("(p j) w -> p j w", j=PACK))
+        for o in range(PASSES):
+            nc.sync.dma_start(scale_table[4 * o : P : 8, :].bitcast(I32), x_scales[o].bitcast(I32))
+        nc.sync.dma_start(h_raw[1][:], hT[512:1024, :].rearrange("(p j) w -> p j w", j=PACK))
+        for o in range(PASSES):
+            nc.sync.dma_start(word_table[o][:].bitcast(I32), x_words[o].rearrange("p n t -> p (n t)").bitcast(I32))
+
+        for t in range(J // P):
+            nc.vector.memset(window[t][:].bitcast(I32), 0)
+
+        nc.scalar.copy(
+            h_grouped[0][:].rearrange("p (c i) t -> p c t i", i=4),
+            h_raw[0][:].rearrange("p t (c i) -> p c t i", i=4),
+        )
+        nc.vector.tensor_copy(scale_picked[:], scale_table[:].indirect(offsets[:]))
+        for q in range(4):
+            nc.scalar.dma_start(
+                x_planes[32 * q : 32 * q + 4, :].bitcast(I32).rearrange("p (o n) -> p o n", o=PASSES),
+                scale_picked[32 * q : 32 * q + 32 : 4, :].bitcast(I32),
+            )
+
+        for o in range(1, PASSES):
+            nc.vector.tensor_copy(
+                h_grouped[o][:].rearrange("p (c i) t -> p c t i", i=4),
+                h_raw[o][:].rearrange("p t (c i) -> p c t i", i=4),
+            )
+        for o in range(PASSES):
+            nc.vector.quantize_mx(
+                out=h_codes[o][:].bitcast(FP8X4), scales=h_planes[o][:], in_=h_grouped[o][:].rearrange("p w j -> p (w j)")
+            )
+
+        nc.vector.tensor_copy(x_codes[0][:], word_table[0][:].indirect(offsets[:]))
+        for c in range(2):
+            nc.vector.tensor_copy(
+                x_codes[1][:, c * HALF : (c + 1) * HALF],
+                word_table[1][:].indirect(offsets[:, c * HALF // 16 : (c + 1) * HALF // 16]),
+            )
+
+        groups = [(0, 0, HALF), (0, HALF, S), (1, 0, S)]
+        banks = [psum.tile([P, 512], F32, name="bank%d" % g) for g in range(len(groups))]
+        for g, (t, a, b) in enumerate(groups):
+            for o in range(PASSES):
+                nc.tensor.matmul_mx(
+                    out=banks[g][:, 0 : b - a],
+                    lhsT=h_codes[o][:, t * P : (t + 1) * P].bitcast(FP8X4),
+                    lhsT_scale=h_planes[o][:, t * P : (t + 1) * P],
+                    rhs=x_codes[o][:, a:b].bitcast(FP8X4),
+                    rhs_scale=x_planes[:, o * S + a : o * S + b],
+                    start=(o == 0),
+                    stop=(o == PASSES - 1),
+                )
+        for g, (t, a, b) in enumerate(groups):
+            nc.scalar.activation(probs[t][:, a:b], banks[g][:, 0 : b - a], SIGMOID)
+            nc.vector.tensor_copy(window[t][:].indirect(offsets[:, a // 16 : b // 16]), probs[t][:, a:b])
+            if b == S:
+                nc.sync.dma_start(out[t * P : (t + 1) * P, :], window[t][:])

@@ -27,44 +27,42 @@ def tile_picked_zvoc_sigmoid_p_kernel(tc, x_words, x_scales, hT, offs, out):
         psum = ctx.enter_context(tc.psum_pool(name="psum", bufs=1))
 
         offsets = keep.tile([P, S // 16], U16, name="offsets")
-        scale_table = keep.tile([P, T], U8, name="scale_table", align_bytes=64)
+        scale_table = keep.tile([P, T], U8, name="scale_table", tag="late", align_bytes=64)
         scale_picked = keep.tile([P, S], U8, name="scale_picked", align_bytes=64)
         x_planes = keep.tile([P, PASSES * S], U8, name="x_planes", align_bytes=64)
         h_raw = [keep.tile([P, PACK, J], F32, name="h_raw%d" % o, align_bytes=64) for o in range(PASSES)]
         h_grouped = [keep.tile([P, J, PACK], BF16, name="h_grouped%d" % o, align_bytes=64) for o in range(PASSES)]
         h_codes = [keep.tile([P, J], U32, name="h_codes%d" % o, align_bytes=64) for o in range(PASSES)]
         h_planes = [keep.tile([P, J], U8, name="h_planes%d" % o, align_bytes=64) for o in range(PASSES)]
-        word_table = [keep.tile([P, T], U32, name="word_table%d" % o, align_bytes=64) for o in range(PASSES)]
+        word_table = [keep.tile([P, T], U32, name="word_table0", align_bytes=64)]
         x_codes = [keep.tile([P, S], U32, name="x_codes%d" % o, align_bytes=64) for o in range(PASSES)]
         window = [keep.tile([P, T], F32, name="window%d" % t, align_bytes=64) for t in range(J // P)]
+        zero = keep.tile([P, 1], F32, name="zero")
         probs = [keep.tile([P, S], F32, name="probs%d" % t, align_bytes=64) for t in range(J // P)]
 
-        nc.vector.memset(scale_table[:].bitcast(I32), 0)
-        nc.vector.memset(x_planes[:].bitcast(I32), 0)
+        nc.gpsimd.memset(zero[:], 0.0)
+        nc.gpsimd.memset(scale_table[0:96, :].bitcast(I32), 0)
+        nc.gpsimd.memset(x_planes[:].bitcast(I32), 0)
 
+        nc.sync.dma_start(scale_table[96:P, :].bitcast(I32), x_scales.bitcast(I32).rearrange("o m n -> m o n"))
         nc.sync.dma_start(offsets[:], offs)
         nc.sync.dma_start(h_raw[0][:], hT[0:512, :].rearrange("(p j) w -> p j w", j=PACK))
-        for o in range(PASSES):
-            nc.sync.dma_start(scale_table[4 * o : P : 8, :].bitcast(I32), x_scales[o].bitcast(I32))
         nc.sync.dma_start(h_raw[1][:], hT[512:1024, :].rearrange("(p j) w -> p j w", j=PACK))
-        for o in range(PASSES):
-            nc.sync.dma_start(word_table[o][:].bitcast(I32), x_words[o].rearrange("p n t -> p (n t)").bitcast(I32))
+        nc.sync.dma_start(word_table[0][:].bitcast(I32), x_words[0].rearrange("p n t -> p (n t)").bitcast(I32))
 
-        for t in range(J // P):
-            nc.vector.memset(window[t][:].bitcast(I32), 0)
+        nc.vector.memset(window[0][:].bitcast(I32), 0)
+        nc.scalar.copy(window[1][:], zero[:].to_broadcast([P, T]))
 
-        nc.scalar.copy(
-            h_grouped[0][:].rearrange("p (c i) t -> p c t i", i=4),
-            h_raw[0][:].rearrange("p t (c i) -> p c t i", i=4),
-        )
         nc.vector.tensor_copy(scale_picked[:], scale_table[:].indirect(offsets[:]))
         for q in range(4):
-            nc.scalar.dma_start(
+            nc.sync.dma_start(
                 x_planes[32 * q : 32 * q + 4, :].bitcast(I32).rearrange("p (o n) -> p o n", o=PASSES),
-                scale_picked[32 * q : 32 * q + 32 : 4, :].bitcast(I32),
+                scale_picked[96 + 8 * q : 96 + 8 * q + 8, :].bitcast(I32),
             )
+        word_table.append(keep.tile([P, T], U32, name="word_table1", tag="late", align_bytes=64))
+        nc.sync.dma_start(word_table[1][:].bitcast(I32), x_words[1].rearrange("p n t -> p (n t)").bitcast(I32))
 
-        for o in range(1, PASSES):
+        for o in range(PASSES):
             nc.vector.tensor_copy(
                 h_grouped[o][:].rearrange("p (c i) t -> p c t i", i=4),
                 h_raw[o][:].rearrange("p t (c i) -> p c t i", i=4),

@@ -27,40 +27,39 @@ def tile_picked_zvoc_sigmoid_p_kernel(tc, x_words, x_scales, hT, offs, out):
         psum = ctx.enter_context(tc.psum_pool(name="psum", bufs=1))
 
         offsets = keep.tile([P, S // 16], U16, name="offsets")
-        scale_table = keep.tile([P, T], U8, name="scale_table", tag="late", align_bytes=64)
+        scale_table = keep.tile([P, T], U8, name="scale_table", align_bytes=64)
         scale_picked = keep.tile([P, S], U8, name="scale_picked", align_bytes=64)
         x_planes = keep.tile([P, PASSES * S], U8, name="x_planes", align_bytes=64)
         h_raw = [keep.tile([P, PACK, J], F32, name="h_raw%d" % o, align_bytes=64) for o in range(PASSES)]
         h_grouped = [keep.tile([P, J, PACK], BF16, name="h_grouped%d" % o, align_bytes=64) for o in range(PASSES)]
         h_codes = [keep.tile([P, J], U32, name="h_codes%d" % o, align_bytes=64) for o in range(PASSES)]
         h_planes = [keep.tile([P, J], U8, name="h_planes%d" % o, align_bytes=64) for o in range(PASSES)]
-        word_table = [keep.tile([P, T], U32, name="word_table0", align_bytes=64)]
+        word_table = [keep.tile([P, T], U32, name="word_table%d" % o, align_bytes=64) for o in range(PASSES)]
         x_codes = [keep.tile([P, S], U32, name="x_codes%d" % o, align_bytes=64) for o in range(PASSES)]
         window = [keep.tile([P, T], F32, name="window%d" % t, align_bytes=64) for t in range(J // P)]
-        zero = keep.tile([P, 1], F32, name="zero")
+        zero = keep.tile([P, P], F32, name="zero", align_bytes=64)
         probs = [keep.tile([P, S], F32, name="probs%d" % t, align_bytes=64) for t in range(J // P)]
 
         nc.gpsimd.memset(zero[:], 0.0)
         nc.gpsimd.memset(scale_table[0:96, :].bitcast(I32), 0)
         nc.gpsimd.memset(x_planes[:].bitcast(I32), 0)
 
-        nc.sync.dma_start(scale_table[96:P, :].bitcast(I32), x_scales.bitcast(I32).rearrange("o m n -> m o n"))
-        nc.sync.dma_start(offsets[:], offs)
+        nc.scalar.dma_start(scale_table[96:P, :].bitcast(I32), x_scales.bitcast(I32).rearrange("o m n -> m o n"))
         nc.sync.dma_start(h_raw[0][:], hT[0:512, :].rearrange("(p j) w -> p j w", j=PACK))
+        nc.sync.dma_start(offsets[:], offs)
         nc.sync.dma_start(h_raw[1][:], hT[512:1024, :].rearrange("(p j) w -> p j w", j=PACK))
-        nc.sync.dma_start(word_table[0][:].bitcast(I32), x_words[0].rearrange("p n t -> p (n t)").bitcast(I32))
+        for o in range(PASSES):
+            nc.sync.dma_start(word_table[o][:].bitcast(I32), x_words[o].rearrange("p n t -> p (n t)").bitcast(I32))
 
         nc.vector.memset(window[0][:].bitcast(I32), 0)
-        nc.scalar.copy(window[1][:], zero[:].to_broadcast([P, T]))
+        nc.scalar.copy(window[1][:], zero[:, 0:1].to_broadcast([P, T]))
 
         nc.vector.tensor_copy(scale_picked[:], scale_table[:].indirect(offsets[:]))
         for q in range(4):
-            nc.sync.dma_start(
+            nc.scalar.dma_start(
                 x_planes[32 * q : 32 * q + 4, :].bitcast(I32).rearrange("p (o n) -> p o n", o=PASSES),
                 scale_picked[96 + 8 * q : 96 + 8 * q + 8, :].bitcast(I32),
             )
-        word_table.append(keep.tile([P, T], U32, name="word_table1", tag="late", align_bytes=64))
-        nc.sync.dma_start(word_table[1][:].bitcast(I32), x_words[1].rearrange("p n t -> p (n t)").bitcast(I32))
 
         for o in range(PASSES):
             nc.vector.tensor_copy(
@@ -79,12 +78,12 @@ def tile_picked_zvoc_sigmoid_p_kernel(tc, x_words, x_scales, hT, offs, out):
                 word_table[1][:].indirect(offsets[:, c * HALF // 16 : (c + 1) * HALF // 16]),
             )
 
-        groups = [(0, 0, HALF), (0, HALF, S), (1, 0, S)]
-        banks = [psum.tile([P, 512], F32, name="bank%d" % g) for g in range(len(groups))]
+        groups = [(0, 0, P), (1, 0, P), (0, P, HALF), (0, HALF, S), (1, P, HALF), (1, HALF, S)]
         for g, (t, a, b) in enumerate(groups):
+            bank = psum.tile([P, 512], F32, name="bank%d" % g, tag="bank%d" % (g % 3))
             for o in range(PASSES):
                 nc.tensor.matmul_mx(
-                    out=banks[g][:, 0 : b - a],
+                    out=bank[:, 0 : b - a],
                     lhsT=h_codes[o][:, t * P : (t + 1) * P].bitcast(FP8X4),
                     lhsT_scale=h_planes[o][:, t * P : (t + 1) * P],
                     rhs=x_codes[o][:, a:b].bitcast(FP8X4),
@@ -92,8 +91,10 @@ def tile_picked_zvoc_sigmoid_p_kernel(tc, x_words, x_scales, hT, offs, out):
                     start=(o == 0),
                     stop=(o == PASSES - 1),
                 )
-        for g, (t, a, b) in enumerate(groups):
-            nc.scalar.activation(probs[t][:, a:b], banks[g][:, 0 : b - a], SIGMOID)
-            nc.vector.tensor_copy(window[t][:].indirect(offsets[:, a // 16 : b // 16]), probs[t][:, a:b])
+            nc.scalar.activation(probs[t][:, a:b], bank[:, 0 : b - a], SIGMOID)
+            if a == 0:
+                nc.vector.tensor_tensor(window[t][:].indirect(offsets[:, a // 16 : b // 16]), probs[t][:, a:b], zero[:], mybir.AluOpType.add)
             if b == S:
+                lo = P
+                nc.vector.tensor_copy(window[t][:].indirect(offsets[:, lo // 16 : S // 16]), probs[t][:, lo:S])
                 nc.sync.dma_start(out[t * P : (t + 1) * P, :], window[t][:])

@@ -27,14 +27,14 @@ def tile_picked_zvoc_sigmoid_p_kernel(tc, x_words, x_scales, hT, offs, out):
         psum = ctx.enter_context(tc.psum_pool(name="psum", bufs=1))
 
         offsets = keep.tile([P, S // 16], U16, name="offsets")
-        scale_table = keep.tile([P, T], U8, name="scale_table", align_bytes=64)
+        scale_table = keep.tile([P, T], U8, name="scale_table", tag="late", align_bytes=64)
         scale_picked = keep.tile([P, S], U8, name="scale_picked", align_bytes=64)
         x_planes = keep.tile([P, PASSES * S], U8, name="x_planes", align_bytes=64)
         h_raw = [keep.tile([P, PACK, J], F32, name="h_raw%d" % o, align_bytes=64) for o in range(PASSES)]
         h_grouped = [keep.tile([P, J, PACK], BF16, name="h_grouped%d" % o, align_bytes=64) for o in range(PASSES)]
         h_codes = [keep.tile([P, J], U32, name="h_codes%d" % o, align_bytes=64) for o in range(PASSES)]
         h_planes = [keep.tile([P, J], U8, name="h_planes%d" % o, align_bytes=64) for o in range(PASSES)]
-        word_table = [keep.tile([P, T], U32, name="word_table%d" % o, align_bytes=64) for o in range(PASSES)]
+        word_table = [keep.tile([P, T], U32, name="word_table0", align_bytes=64)]
         x_codes = [keep.tile([P, S], U32, name="x_codes%d" % o, align_bytes=64) for o in range(PASSES)]
         window = [keep.tile([P, T], F32, name="window%d" % t, align_bytes=64) for t in range(J // P)]
         zero = keep.tile([P, P], F32, name="zero", align_bytes=64)
@@ -44,22 +44,24 @@ def tile_picked_zvoc_sigmoid_p_kernel(tc, x_words, x_scales, hT, offs, out):
         nc.gpsimd.memset(scale_table[0:96, :].bitcast(I32), 0)
         nc.gpsimd.memset(x_planes[:].bitcast(I32), 0)
 
-        nc.scalar.dma_start(scale_table[96:P, :].bitcast(I32), x_scales.bitcast(I32).rearrange("o m n -> m o n"))
-        nc.sync.dma_start(h_raw[0][:], hT[0:512, :].rearrange("(p j) w -> p j w", j=PACK))
+        nc.sync.dma_start(scale_table[96:P, :].bitcast(I32), x_scales.bitcast(I32).rearrange("o m n -> m o n"))
         nc.sync.dma_start(offsets[:], offs)
+        nc.sync.dma_start(h_raw[0][:], hT[0:512, :].rearrange("(p j) w -> p j w", j=PACK))
         nc.sync.dma_start(h_raw[1][:], hT[512:1024, :].rearrange("(p j) w -> p j w", j=PACK))
-        for o in range(PASSES):
-            nc.sync.dma_start(word_table[o][:].bitcast(I32), x_words[o].rearrange("p n t -> p (n t)").bitcast(I32))
+        nc.sync.dma_start(word_table[0][:].bitcast(I32), x_words[0].rearrange("p n t -> p (n t)").bitcast(I32))
 
-        nc.vector.memset(window[0][:].bitcast(I32), 0)
+        nc.vector.memset(window[0][:, 0 : T // 2].bitcast(I32), 0)
+        nc.scalar.copy(window[0][:, T // 2 : T], zero[:, 0:1].to_broadcast([P, T // 2]))
         nc.scalar.copy(window[1][:], zero[:, 0:1].to_broadcast([P, T]))
 
         nc.vector.tensor_copy(scale_picked[:], scale_table[:].indirect(offsets[:]))
         for q in range(4):
-            nc.scalar.dma_start(
+            nc.sync.dma_start(
                 x_planes[32 * q : 32 * q + 4, :].bitcast(I32).rearrange("p (o n) -> p o n", o=PASSES),
                 scale_picked[96 + 8 * q : 96 + 8 * q + 8, :].bitcast(I32),
             )
+        word_table.append(keep.tile([P, T], U32, name="word_table1", tag="late", align_bytes=64))
+        nc.sync.dma_start(word_table[1][:].bitcast(I32), x_words[1].rearrange("p n t -> p (n t)").bitcast(I32))
 
         for o in range(PASSES):
             nc.vector.tensor_copy(

@@ -30,15 +30,46 @@ def tile_picked_zvoc_sigmoid_p_kernel(tc, x_words, x_scales, hT, offs, out):
         scale_table = keep.tile([P, T], U8, name="scale_table", tag="late", align_bytes=64)
         scale_picked = keep.tile([P, S], U8, name="scale_picked", align_bytes=64)
         x_planes = keep.tile([P, PASSES * S], U8, name="x_planes", align_bytes=64)
-        h_raw = [keep.tile([P, PACK, J], F32, name="h_raw%d" % o, align_bytes=64) for o in range(PASSES)]
-        h_grouped = [keep.tile([P, J, PACK], BF16, name="h_grouped%d" % o, align_bytes=64) for o in range(PASSES)]
-        h_codes = [keep.tile([P, J], U32, name="h_codes%d" % o, align_bytes=64) for o in range(PASSES)]
-        h_planes = [keep.tile([P, J], U8, name="h_planes%d" % o, align_bytes=64) for o in range(PASSES)]
-        word_table = [keep.tile([P, T], U32, name="word_table0", align_bytes=64)]
+        h_raw = [[keep.tile([P, PACK, P], F32, name="h_raw0%d" % o, align_bytes=64)[:] for o in range(PASSES)]]
+        h_grouped = [keep.tile([P, PASSES * P * PACK], BF16, name="h_grouped%d" % t, align_bytes=64) for t in range(J // P)]
+        h_codes = [keep.tile([P, PASSES * P], U32, name="h_codes%d" % t, align_bytes=64) for t in range(J // P)]
+        h_planes = [keep.tile([P, PASSES * P], U8, name="h_planes%d" % t, align_bytes=64) for t in range(J // P)]
+        word_table = [keep.tile([P, T], U32, name="word_table%d" % o, align_bytes=64) for o in range(PASSES)]
         x_codes = [keep.tile([P, S], U32, name="x_codes%d" % o, align_bytes=64) for o in range(PASSES)]
         window = [keep.tile([P, T], F32, name="window%d" % t, align_bytes=64) for t in range(J // P)]
         zero = keep.tile([P, P], F32, name="zero", align_bytes=64)
-        probs = [keep.tile([P, S], F32, name="probs%d" % t, align_bytes=64) for t in range(J // P)]
+
+        def load_h(t, o):
+            nc.sync.dma_start(h_raw[t][o], hT[o * 512 : (o + 1) * 512, t * P : (t + 1) * P].rearrange("(p j) w -> p j w", j=PACK))
+
+        def load_words(o):
+            nc.sync.dma_start(word_table[o][:].bitcast(I32), x_words[o].rearrange("p n t -> p (n t)").bitcast(I32))
+
+        def interleave(copy, t, o):
+            copy(
+                h_grouped[t][:, o * P * PACK : (o + 1) * P * PACK].rearrange("p (c i t) -> p c t i", i=4, t=PACK),
+                h_raw[t][o].rearrange("p t (c i) -> p c t i", i=4),
+            )
+
+        def quantise(t):
+            nc.vector.quantize_mx(out=h_codes[t][:].bitcast(FP8X4), scales=h_planes[t][:], in_=h_grouped[t][:])
+
+        def product(t, a, b, probs):
+            bank = psum.tile([P, 512], F32, name="bank%d_%d" % (t, a))
+            for o in range(PASSES):
+                nc.tensor.matmul_mx(
+                    out=bank[:, 0 : b - a],
+                    lhsT=h_codes[t][:, o * P : (o + 1) * P].bitcast(FP8X4),
+                    lhsT_scale=h_planes[t][:, o * P : (o + 1) * P],
+                    rhs=x_codes[o][:, a:b].bitcast(FP8X4),
+                    rhs_scale=x_planes[:, o * S + a : o * S + b],
+                    start=(o == 0),
+                    stop=(o == PASSES - 1),
+                )
+            nc.scalar.activation(probs, bank[:, 0 : b - a], SIGMOID)
+
+        def scatter(t, a, b, probs):
+            nc.vector.tensor_copy(window[t][:].indirect(offsets[:, a // 16 : b // 16]), probs)
 
         nc.gpsimd.memset(zero[:], 0.0)
         nc.gpsimd.memset(scale_table[0:96, :].bitcast(I32), 0)
@@ -46,12 +77,12 @@ def tile_picked_zvoc_sigmoid_p_kernel(tc, x_words, x_scales, hT, offs, out):
 
         nc.sync.dma_start(scale_table[96:P, :].bitcast(I32), x_scales.bitcast(I32).rearrange("o m n -> m o n"))
         nc.sync.dma_start(offsets[:], offs)
-        nc.sync.dma_start(h_raw[0][:], hT[0:512, :].rearrange("(p j) w -> p j w", j=PACK))
-        nc.sync.dma_start(h_raw[1][:], hT[512:1024, :].rearrange("(p j) w -> p j w", j=PACK))
-        nc.sync.dma_start(word_table[0][:].bitcast(I32), x_words[0].rearrange("p n t -> p (n t)").bitcast(I32))
+        load_h(0, 0)
+        load_h(0, 1)
+        load_words(0)
+        load_words(1)
 
-        nc.vector.memset(window[0][:, 0 : T // 2].bitcast(I32), 0)
-        nc.scalar.copy(window[0][:, T // 2 : T], zero[:, 0:1].to_broadcast([P, T // 2]))
+        nc.vector.memset(window[0][:].bitcast(I32), 0)
         nc.scalar.copy(window[1][:], zero[:, 0:1].to_broadcast([P, T]))
 
         nc.vector.tensor_copy(scale_picked[:], scale_table[:].indirect(offsets[:]))
@@ -60,18 +91,15 @@ def tile_picked_zvoc_sigmoid_p_kernel(tc, x_words, x_scales, hT, offs, out):
                 x_planes[32 * q : 32 * q + 4, :].bitcast(I32).rearrange("p (o n) -> p o n", o=PASSES),
                 scale_picked[96 + 8 * q : 96 + 8 * q + 8, :].bitcast(I32),
             )
-        word_table.append(keep.tile([P, T], U32, name="word_table1", tag="late", align_bytes=64))
-        nc.sync.dma_start(word_table[1][:].bitcast(I32), x_words[1].rearrange("p n t -> p (n t)").bitcast(I32))
+
+        h_late = keep.tile([P, PASSES * PACK * P], F32, name="h_late", tag="late", align_bytes=64)
+        h_raw.append([h_late[:, o * PACK * P : (o + 1) * PACK * P].rearrange("p (j w) -> p j w", j=PACK) for o in range(PASSES)])
+        load_h(1, 0)
+        load_h(1, 1)
 
         for o in range(PASSES):
-            nc.vector.tensor_copy(
-                h_grouped[o][:].rearrange("p (c i) t -> p c t i", i=4),
-                h_raw[o][:].rearrange("p t (c i) -> p c t i", i=4),
-            )
-        for o in range(PASSES):
-            nc.vector.quantize_mx(
-                out=h_codes[o][:].bitcast(FP8X4), scales=h_planes[o][:], in_=h_grouped[o][:].rearrange("p w j -> p (w j)")
-            )
+            interleave(nc.vector.tensor_copy, 0, o)
+        quantise(0)
 
         nc.vector.tensor_copy(x_codes[0][:], word_table[0][:].indirect(offsets[:]))
         for c in range(2):
@@ -80,23 +108,19 @@ def tile_picked_zvoc_sigmoid_p_kernel(tc, x_words, x_scales, hT, offs, out):
                 word_table[1][:].indirect(offsets[:, c * HALF // 16 : (c + 1) * HALF // 16]),
             )
 
-        groups = [(0, 0, P), (1, 0, P), (0, P, HALF), (0, HALF, S), (1, P, HALF), (1, HALF, S)]
-        for g, (t, a, b) in enumerate(groups):
-            bank = psum.tile([P, 512], F32, name="bank%d" % g, tag="bank%d" % (g % 3))
-            for o in range(PASSES):
-                nc.tensor.matmul_mx(
-                    out=bank[:, 0 : b - a],
-                    lhsT=h_codes[o][:, t * P : (t + 1) * P].bitcast(FP8X4),
-                    lhsT_scale=h_planes[o][:, t * P : (t + 1) * P],
-                    rhs=x_codes[o][:, a:b].bitcast(FP8X4),
-                    rhs_scale=x_planes[:, o * S + a : o * S + b],
-                    start=(o == 0),
-                    stop=(o == PASSES - 1),
-                )
-            nc.scalar.activation(probs[t][:, a:b], bank[:, 0 : b - a], SIGMOID)
-            if a == 0:
-                nc.vector.tensor_tensor(window[t][:].indirect(offsets[:, a // 16 : b // 16]), probs[t][:, a:b], zero[:], mybir.AluOpType.add)
-            if b == S:
-                lo = P
-                nc.vector.tensor_copy(window[t][:].indirect(offsets[:, lo // 16 : S // 16]), probs[t][:, lo:S])
-                nc.sync.dma_start(out[t * P : (t + 1) * P, :], window[t][:])
+        first = keep.tile([P, P], F32, name="first", align_bytes=64)
+        product(0, 0, P, first[:])
+        interleave(nc.vector.tensor_copy, 1, 0)
+        nc.vector.tensor_tensor(window[0][:].indirect(offsets[:, 0 : P // 16]), first[:], zero[:], mybir.AluOpType.add)
+        interleave(nc.scalar.copy, 1, 1)
+        quantise(1)
+        second = keep.tile([P, S - P], F32, name="second", tag="late", align_bytes=64)
+        product(0, P, HALF, second[:, 0 : HALF - P])
+        product(0, HALF, S, second[:, HALF - P : S - P])
+        scatter(0, P, S, second[:])
+        nc.sync.dma_start(out[0:P, :], window[0][:])
+        last = keep.tile([P, S], F32, name="last", align_bytes=64)
+        for c in range(2):
+            product(1, c * HALF, (c + 1) * HALF, last[:, c * HALF : (c + 1) * HALF])
+        scatter(1, 0, S, last[:])
+        nc.sync.dma_start(out[P:J, :], window[1][:])

@@ -40,7 +40,8 @@ def tile_picked_zvoc_sigmoid_p_kernel(tc, x_words, x_scales, hT, offs, out):
         zero = keep.tile([P, P], F32, name="zero", align_bytes=64)
 
         def load_h(t, o):
-            nc.sync.dma_start(h_raw[t][o], hT[o * 512 : (o + 1) * 512, t * P : (t + 1) * P].rearrange("(p j) w -> p j w", j=PACK))
+            queue = nc.scalar if t == 0 else nc.sync
+            queue.dma_start(h_raw[t][o], hT[o * 512 : (o + 1) * 512, t * P : (t + 1) * P].rearrange("(p j) w -> p j w", j=PACK))
 
         def load_words(o):
             nc.sync.dma_start(word_table[o][:].bitcast(I32), x_words[o].rearrange("p n t -> p (n t)").bitcast(I32))

@@ -57,15 +57,16 @@ def tile_picked_zvoc_sigmoid_p_kernel(tc, x_words, x_scales, hT, offs, out):
 
         def product(t, a, b, probs):
             bank = psum.tile([P, 512], F32, name="bank%d_%d" % (t, a))
-            for o in range(PASSES):
+            order = list(range(PASSES)) if (t, a) == (0, 0) or t == 1 else list(reversed(range(PASSES)))
+            for o in order:
                 nc.tensor.matmul_mx(
                     out=bank[:, 0 : b - a],
                     lhsT=h_codes[t][:, o * P : (o + 1) * P].bitcast(FP8X4),
                     lhsT_scale=h_planes[t][:, o * P : (o + 1) * P],
                     rhs=x_codes[o][:, a:b].bitcast(FP8X4),
                     rhs_scale=x_planes[:, o * S + a : o * S + b],
-                    start=(o == 0),
-                    stop=(o == PASSES - 1),
+                    start=(o == order[0]),
+                    stop=(o == order[-1]),
                 )
             nc.scalar.activation(probs, bank[:, 0 : b - a], SIGMOID)
 
@@ -87,7 +88,7 @@ def tile_picked_zvoc_sigmoid_p_kernel(tc, x_words, x_scales, hT, offs, out):
         nc.scalar.copy(window[1][:], zero[:, 0:1].to_broadcast([P, T]))
 
         nc.vector.tensor_copy(scale_picked[:], scale_table[:].indirect(offsets[:]))
-        for q in range(4):
+        for q in (0, 2, 1, 3):
             nc.sync.dma_start(
                 x_planes[32 * q : 32 * q + 4, :].bitcast(I32).rearrange("p (o n) -> p o n", o=PASSES),
                 scale_picked[96 + 8 * q : 96 + 8 * q + 8, :].bitcast(I32),

@@ -18,74 +18,77 @@ P = 128
 PACK = 4
 PASSES = K // (P * PACK)
 HALF = S // 2
+FIRST = 192
+BETWEEN = 96
 
 
 def tile_picked_zvoc_sigmoid_p_kernel(tc, x_words, x_scales, hT, offs, out):
     nc = tc.nc
     with ExitStack() as ctx:
         keep = ctx.enter_context(tc.tile_pool(name="keep", bufs=1))
+        reuse = ctx.enter_context(tc.tile_pool(name="reuse", bufs=1))
         psum = ctx.enter_context(tc.psum_pool(name="psum", bufs=1))
 
+        def sbuf(name, shape, dtype, tag=None):
+            return keep.tile(shape, dtype, name=name, tag=tag or name, align_bytes=64)
+
         offsets = keep.tile([P, S // 16], U16, name="offsets")
-        scale_table = keep.tile([P, T], U8, name="scale_table", tag="late", align_bytes=64)
-        scale_picked = keep.tile([P, S], U8, name="scale_picked", align_bytes=64)
-        x_planes = keep.tile([P, PASSES * S], U8, name="x_planes", align_bytes=64)
-        h_raw = [[keep.tile([P, PACK, P], F32, name="h_raw0%d" % o, align_bytes=64)[:] for o in range(PASSES)]]
-        h_grouped = [keep.tile([P, PASSES * P * PACK], BF16, name="h_grouped%d" % t, align_bytes=64) for t in range(J // P)]
-        h_codes = [keep.tile([P, PASSES * P], U32, name="h_codes%d" % t, align_bytes=64) for t in range(J // P)]
-        h_planes = [keep.tile([P, PASSES * P], U8, name="h_planes%d" % t, align_bytes=64) for t in range(J // P)]
-        word_table = [keep.tile([P, T], U32, name="word_table%d" % o, align_bytes=64) for o in range(PASSES)]
-        x_codes = [keep.tile([P, S], U32, name="x_codes%d" % o, align_bytes=64) for o in range(PASSES)]
-        window = [keep.tile([P, T], F32, name="window%d" % t, align_bytes=64) for t in range(J // P)]
-        zero = keep.tile([P, P], F32, name="zero", align_bytes=64)
+        scale_table = reuse.tile([P, T], U8, name="scale_table", offset=1024)
+        scale_picked = sbuf("scale_picked", [P, S], U8)
+        x_planes = sbuf("x_planes", [P, PASSES * S], U8)
+        word_table = [sbuf("word_table%d" % o, [P, T], U32) for o in range(PASSES)]
+        x_codes = [sbuf("x_codes%d" % o, [P, S], U32) for o in range(PASSES)]
+        window = [sbuf("window%d" % t, [P, T], F32) for t in range(J // P)]
+        zero = sbuf("zero", [P, FIRST], F32)
+        far_below = sbuf("far_below", [P, 1], F32)
+        h_raw = {(0, o): sbuf("h_raw0%d" % o, [P, PACK, P], F32)[:] for o in range(PASSES)}
+        pieces = [(t, o) for t in range(J // P) for o in range(PASSES)]
+        h_grouped = {k: sbuf("h_grouped%d%d" % k, [P, P * PACK], BF16) for k in pieces}
+        h_codes = {k: sbuf("h_codes%d%d" % k, [P, P], U32) for k in pieces}
+        h_planes = {k: sbuf("h_planes%d%d" % k, [P, P], U8) for k in pieces}
 
         def load_h(t, o):
             queue = nc.scalar if t == 0 else nc.sync
-            queue.dma_start(h_raw[t][o], hT[o * 512 : (o + 1) * 512, t * P : (t + 1) * P].rearrange("(p j) w -> p j w", j=PACK))
-
-        def load_words(o):
-            nc.sync.dma_start(word_table[o][:].bitcast(I32), x_words[o].rearrange("p n t -> p (n t)").bitcast(I32))
+            queue.dma_start(h_raw[t, o], hT[o * 512 : (o + 1) * 512, t * P : (t + 1) * P].rearrange("(p j) w -> p j w", j=PACK))
 
         def interleave(copy, t, o):
             copy(
-                h_grouped[t][:, o * P * PACK : (o + 1) * P * PACK].rearrange("p (c i t) -> p c t i", i=4, t=PACK),
-                h_raw[t][o].rearrange("p t (c i) -> p c t i", i=4),
+                h_grouped[t, o][:].rearrange("p (c i t) -> p c t i", i=4, t=PACK),
+                h_raw[t, o].rearrange("p t (c i) -> p c t i", i=4),
             )
 
-        def quantise(t):
-            nc.vector.quantize_mx(out=h_codes[t][:].bitcast(FP8X4), scales=h_planes[t][:], in_=h_grouped[t][:])
+        def quantise(t, o):
+            nc.vector.quantize_mx(out=h_codes[t, o][:].bitcast(FP8X4), scales=h_planes[t, o][:], in_=h_grouped[t, o][:])
 
-        def product(t, a, b, probs):
-            bank = psum.tile([P, 512], F32, name="bank%d_%d" % (t, a))
-            order = list(range(PASSES)) if (t, a) == (0, 0) or t == 1 else list(reversed(range(PASSES)))
-            for o in order:
+        def product(t, a, b, logits):
+            for o in range(PASSES):
                 nc.tensor.matmul_mx(
-                    out=bank[:, 0 : b - a],
-                    lhsT=h_codes[t][:, o * P : (o + 1) * P].bitcast(FP8X4),
-                    lhsT_scale=h_planes[t][:, o * P : (o + 1) * P],
+                    out=logits,
+                    lhsT=h_codes[t, o][:].bitcast(FP8X4),
+                    lhsT_scale=h_planes[t, o][:],
                     rhs=x_codes[o][:, a:b].bitcast(FP8X4),
                     rhs_scale=x_planes[:, o * S + a : o * S + b],
-                    start=(o == order[0]),
-                    stop=(o == order[-1]),
+                    start=(o == 0),
+                    stop=(o == PASSES - 1),
                 )
-            nc.scalar.activation(probs, bank[:, 0 : b - a], SIGMOID)
 
         def scatter(t, a, b, probs):
             nc.vector.tensor_copy(window[t][:].indirect(offsets[:, a // 16 : b // 16]), probs)
 
-        nc.gpsimd.memset(zero[:], 0.0)
+        nc.gpsimd.memset(far_below[:], -256.0)
         nc.gpsimd.memset(scale_table[0:96, :].bitcast(I32), 0)
         nc.gpsimd.memset(x_planes[:].bitcast(I32), 0)
+        nc.gpsimd.memset(zero[:], 0.0)
 
         nc.sync.dma_start(scale_table[96:P, :].bitcast(I32), x_scales.bitcast(I32).rearrange("o m n -> m o n"))
         nc.sync.dma_start(offsets[:], offs)
         load_h(0, 0)
         load_h(0, 1)
-        load_words(0)
-        load_words(1)
+        for o in range(PASSES):
+            nc.sync.dma_start(word_table[o][:].bitcast(I32), x_words[o].rearrange("p n t -> p (n t)").bitcast(I32))
 
         nc.vector.memset(window[0][:].bitcast(I32), 0)
-        nc.scalar.copy(window[1][:], zero[:, 0:1].to_broadcast([P, T]))
+        nc.scalar.activation(window[1][:], far_below[:, 0:1].to_broadcast([P, T]), SIGMOID)
 
         nc.vector.tensor_copy(scale_picked[:], scale_table[:].indirect(offsets[:]))
         for q in (0, 2, 1, 3):
@@ -94,35 +97,45 @@ def tile_picked_zvoc_sigmoid_p_kernel(tc, x_words, x_scales, hT, offs, out):
                 scale_picked[96 + 8 * q : 96 + 8 * q + 8, :].bitcast(I32),
             )
 
-        h_late = keep.tile([P, PASSES * PACK * P], F32, name="h_late", tag="late", align_bytes=64)
-        h_raw.append([h_late[:, o * PACK * P : (o + 1) * PACK * P].rearrange("p (j w) -> p j w", j=PACK) for o in range(PASSES)])
-        load_h(1, 0)
-        load_h(1, 1)
+        for o in range(PASSES):
+            h_raw[1, o] = reuse.tile([P, PACK, P], F32, name="h_raw1%d" % o, offset=2048 * o)[:]
+            load_h(1, o)
 
         for o in range(PASSES):
             interleave(nc.vector.tensor_copy, 0, o)
-        quantise(0)
-
+        for o in range(PASSES):
+            quantise(0, o)
         nc.vector.tensor_copy(x_codes[0][:], word_table[0][:].indirect(offsets[:]))
         for c in range(2):
             nc.vector.tensor_copy(
                 x_codes[1][:, c * HALF : (c + 1) * HALF],
                 word_table[1][:].indirect(offsets[:, c * HALF // 16 : (c + 1) * HALF // 16]),
             )
+        interleave(nc.scalar.copy, 1, 0)
+        interleave(nc.vector.tensor_copy, 1, 1)
+        quantise(1, 0)
+        quantise(1, 1)
 
-        first = keep.tile([P, P], F32, name="first", align_bytes=64)
-        product(0, 0, P, first[:])
-        interleave(nc.vector.tensor_copy, 1, 0)
-        nc.vector.tensor_tensor(window[0][:].indirect(offsets[:, 0 : P // 16]), first[:], zero[:], mybir.AluOpType.add)
-        interleave(nc.scalar.copy, 1, 1)
-        quantise(1)
-        second = keep.tile([P, S - P], F32, name="second", tag="late", align_bytes=64)
-        product(0, P, HALF, second[:, 0 : HALF - P])
-        product(0, HALF, S, second[:, HALF - P : S - P])
-        scatter(0, P, S, second[:])
+        probs = [reuse.tile([P, S], F32, name="probs0", offset=0), sbuf("probs1", [P, S], F32)]
+        opening = psum.tile([P, 512], F32, name="opening")
+        product(0, 0, HALF, opening[:, 0:HALF])
+        nc.scalar.activation(probs[0][:, 0:FIRST], opening[:, 0:FIRST], SIGMOID)
+        nc.vector.tensor_tensor(window[0][:].indirect(offsets[:, 0 : FIRST // 16]), probs[0][:, 0:FIRST], zero[:], mybir.AluOpType.add)
+        nc.scalar.activation(probs[0][:, FIRST:HALF], opening[:, FIRST:HALF], SIGMOID)
+
+        bank = psum.tile([P, 512], F32, name="bank_a", tag="turn")
+        product(0, HALF, S, bank[:, HALF:S])
+        product(1, 0, P, bank[:, 0:P])
+        nc.scalar.activation(probs[1][:, 0:P], bank[:, 0:P], SIGMOID)
+        nc.vector.tensor_tensor(window[1][:].indirect(offsets[:, 0 : BETWEEN // 16]), probs[1][:, 0:BETWEEN], zero[:, 0:BETWEEN], mybir.AluOpType.add)
+
+        nc.scalar.activation(probs[0][:, HALF:S], bank[:, HALF:S], SIGMOID)
+        scatter(0, FIRST, S, probs[0][:, FIRST:S])
         nc.sync.dma_start(out[0:P, :], window[0][:])
-        last = keep.tile([P, S], F32, name="last", align_bytes=64)
-        for c in range(2):
-            product(1, c * HALF, (c + 1) * HALF, last[:, c * HALF : (c + 1) * HALF])
-        scatter(1, 0, S, last[:])
+
+        bank = psum.tile([P, 512], F32, name="bank_c", tag="turn")
+        product(1, P, HALF, bank[:, P:HALF])
+        product(1, HALF, S, bank[:, HALF:S])
+        nc.scalar.activation(probs[1][:, P:S], bank[:, P:S], SIGMOID)
+        scatter(1, BETWEEN, S, probs[1][:, BETWEEN:S])
         nc.sync.dma_start(out[P:J, :], window[1][:])

@@ -18,7 +18,6 @@ P = 128
 PACK = 4
 PASSES = K // (P * PACK)
 HALF = S // 2
-FIRST = 192
 BETWEEN = 96
 
 
@@ -39,7 +38,7 @@ def tile_picked_zvoc_sigmoid_p_kernel(tc, x_words, x_scales, hT, offs, out):
         word_table = [sbuf("word_table%d" % o, [P, T], U32) for o in range(PASSES)]
         x_codes = [sbuf("x_codes%d" % o, [P, S], U32) for o in range(PASSES)]
         window = [sbuf("window%d" % t, [P, T], F32) for t in range(J // P)]
-        zero = sbuf("zero", [P, FIRST], F32)
+        zero = sbuf("zero", [P, BETWEEN], F32)
         far_below = sbuf("far_below", [P, 1], F32)
         h_raw = {(0, o): sbuf("h_raw0%d" % o, [P, PACK, P], F32)[:] for o in range(PASSES)}
         pieces = [(t, o) for t in range(J // P) for o in range(PASSES)]
@@ -119,18 +118,17 @@ def tile_picked_zvoc_sigmoid_p_kernel(tc, x_words, x_scales, hT, offs, out):
         probs = [reuse.tile([P, S], F32, name="probs0", offset=0), sbuf("probs1", [P, S], F32)]
         opening = psum.tile([P, 512], F32, name="opening")
         product(0, 0, HALF, opening[:, 0:HALF])
-        nc.scalar.activation(probs[0][:, 0:FIRST], opening[:, 0:FIRST], SIGMOID)
-        nc.vector.tensor_tensor(window[0][:].indirect(offsets[:, 0 : FIRST // 16]), probs[0][:, 0:FIRST], zero[:], mybir.AluOpType.add)
-        nc.scalar.activation(probs[0][:, FIRST:HALF], opening[:, FIRST:HALF], SIGMOID)
+        nc.scalar.activation(probs[0][:, 0:HALF], opening[:, 0:HALF], SIGMOID)
+        scatter(0, 0, HALF, probs[0][:, 0:HALF])
 
         bank = psum.tile([P, 512], F32, name="bank_a", tag="turn")
         product(0, HALF, S, bank[:, HALF:S])
         product(1, 0, P, bank[:, 0:P])
         nc.scalar.activation(probs[1][:, 0:P], bank[:, 0:P], SIGMOID)
-        nc.vector.tensor_tensor(window[1][:].indirect(offsets[:, 0 : BETWEEN // 16]), probs[1][:, 0:BETWEEN], zero[:, 0:BETWEEN], mybir.AluOpType.add)
+        nc.vector.tensor_tensor(window[1][:].indirect(offsets[:, 0 : BETWEEN // 16]), probs[1][:, 0:BETWEEN], zero[:], mybir.AluOpType.add)
 
         nc.scalar.activation(probs[0][:, HALF:S], bank[:, HALF:S], SIGMOID)
-        scatter(0, FIRST, S, probs[0][:, FIRST:S])
+        scatter(0, HALF, S, probs[0][:, HALF:S])
         nc.sync.dma_start(out[0:P, :], window[0][:])
 
         bank = psum.tile([P, 512], F32, name="bank_c", tag="turn")

@@ -131,7 +131,7 @@ def tile_picked_zvoc_sigmoid_p_kernel(tc, x_words, x_scales, hT, offs, out):
         scatter(0, HALF, S, probs[0][:, HALF:S])
         nc.sync.dma_start(out[0:P, :], window[0][:])
 
-        bank = psum.tile([P, 512], F32, name="bank_c", tag="turn")
+        bank = psum.tile([P, 512], F32, name="bank_c", tag="opening")
         product(1, P, HALF, bank[:, P:HALF])
         product(1, HALF, S, bank[:, HALF:S])
         nc.scalar.activation(probs[1][:, P:S], bank[:, P:S], SIGMOID)

@@ -19,6 +19,7 @@ PACK = 4
 PASSES = K // (P * PACK)
 HALF = S // 2
 BETWEEN = 96
+SHARE = 96
 
 
 def tile_picked_zvoc_sigmoid_p_kernel(tc, x_words, x_scales, hT, offs, out):
@@ -50,10 +51,10 @@ def tile_picked_zvoc_sigmoid_p_kernel(tc, x_words, x_scales, hT, offs, out):
             queue = nc.scalar if t == 0 else nc.sync
             queue.dma_start(h_raw[t, o], hT[o * 512 : (o + 1) * 512, t * P : (t + 1) * P].rearrange("(p j) w -> p j w", j=PACK))
 
-        def interleave(copy, t, o):
+        def interleave(copy, t, o, lo=0, hi=P):
             copy(
-                h_grouped[t, o][:].rearrange("p (c i t) -> p c t i", i=4, t=PACK),
-                h_raw[t, o].rearrange("p t (c i) -> p c t i", i=4),
+                h_grouped[t, o][:, lo * PACK : hi * PACK].rearrange("p (c i t) -> p c t i", i=4, t=PACK),
+                h_raw[t, o][:, :, lo:hi].rearrange("p t (c i) -> p c t i", i=4),
             )
 
         def quantise(t, o):
@@ -111,7 +112,8 @@ def tile_picked_zvoc_sigmoid_p_kernel(tc, x_words, x_scales, hT, offs, out):
                 word_table[1][:].indirect(offsets[:, c * HALF // 16 : (c + 1) * HALF // 16]),
             )
         interleave(nc.scalar.copy, 1, 0)
-        interleave(nc.vector.tensor_copy, 1, 1)
+        interleave(nc.vector.tensor_copy, 1, 1, 0, SHARE)
+        interleave(nc.scalar.copy, 1, 1, SHARE, P)
         quantise(1, 0)
         quantise(1, 1)
 

@@ -13,13 +13,14 @@ U16 = mybir.dt.uint16
 U8 = mybir.dt.uint8
 FP8X4 = mybir.dt.float8_e4m3fn_x4
 SIGMOID = mybir.ActivationFunctionType.Sigmoid
+COPY = mybir.ActivationFunctionType.Copy
 
 P = 128
 PACK = 4
 PASSES = K // (P * PACK)
 HALF = S // 2
-BETWEEN = 96
-SHARE = 96
+FIRST_CUTS = [(0, 256), (256, 384), (384, 512)]
+SECOND_CUTS = [(0, HALF), (HALF, S)]
 
 
 def tile_picked_zvoc_sigmoid_p_kernel(tc, x_words, x_scales, hT, offs, out):
@@ -29,8 +30,8 @@ def tile_picked_zvoc_sigmoid_p_kernel(tc, x_words, x_scales, hT, offs, out):
         reuse = ctx.enter_context(tc.tile_pool(name="reuse", bufs=1))
         psum = ctx.enter_context(tc.psum_pool(name="psum", bufs=1))
 
-        def sbuf(name, shape, dtype, tag=None):
-            return keep.tile(shape, dtype, name=name, tag=tag or name, align_bytes=64)
+        def sbuf(name, shape, dtype):
+            return keep.tile(shape, dtype, name=name, align_bytes=64)
 
         offsets = keep.tile([P, S // 16], U16, name="offsets")
         scale_table = reuse.tile([P, T], U8, name="scale_table", offset=1024)
@@ -39,7 +40,6 @@ def tile_picked_zvoc_sigmoid_p_kernel(tc, x_words, x_scales, hT, offs, out):
         word_table = [sbuf("word_table%d" % o, [P, T], U32) for o in range(PASSES)]
         x_codes = [sbuf("x_codes%d" % o, [P, S], U32) for o in range(PASSES)]
         window = [sbuf("window%d" % t, [P, T], F32) for t in range(J // P)]
-        zero = sbuf("zero", [P, BETWEEN], F32)
         far_below = sbuf("far_below", [P, 1], F32)
         h_raw = {(0, o): sbuf("h_raw0%d" % o, [P, PACK, P], F32)[:] for o in range(PASSES)}
         pieces = [(t, o) for t in range(J // P) for o in range(PASSES)]
@@ -51,34 +51,32 @@ def tile_picked_zvoc_sigmoid_p_kernel(tc, x_words, x_scales, hT, offs, out):
             queue = nc.scalar if t == 0 else nc.sync
             queue.dma_start(h_raw[t, o], hT[o * 512 : (o + 1) * 512, t * P : (t + 1) * P].rearrange("(p j) w -> p j w", j=PACK))
 
-        def interleave(copy, t, o, lo=0, hi=P):
+        def interleave(copy, t, o):
             copy(
-                h_grouped[t, o][:, lo * PACK : hi * PACK].rearrange("p (c i t) -> p c t i", i=4, t=PACK),
-                h_raw[t, o][:, :, lo:hi].rearrange("p t (c i) -> p c t i", i=4),
+                h_grouped[t, o][:].rearrange("p (c i t) -> p c t i", i=4, t=PACK),
+                h_raw[t, o].rearrange("p t (c i) -> p c t i", i=4),
             )
 
         def quantise(t, o):
             nc.vector.quantize_mx(out=h_codes[t, o][:].bitcast(FP8X4), scales=h_planes[t, o][:], in_=h_grouped[t, o][:])
 
-        def product(t, a, b, logits):
-            for o in range(PASSES):
-                nc.tensor.matmul_mx(
-                    out=logits,
-                    lhsT=h_codes[t, o][:].bitcast(FP8X4),
-                    lhsT_scale=h_planes[t, o][:],
-                    rhs=x_codes[o][:, a:b].bitcast(FP8X4),
-                    rhs_scale=x_planes[:, o * S + a : o * S + b],
-                    start=(o == 0),
-                    stop=(o == PASSES - 1),
-                )
+        def one_pass(t, o, a, b, logits):
+            nc.tensor.matmul_mx(
+                out=logits,
+                lhsT=h_codes[t, o][:].bitcast(FP8X4),
+                lhsT_scale=h_planes[t, o][:],
+                rhs=x_codes[o][:, a:b].bitcast(FP8X4),
+                rhs_scale=x_planes[:, o * S + a : o * S + b],
+                start=(o == 0),
+                stop=(o == PASSES - 1),
+            )
 
-        def scatter(t, a, b, probs):
-            nc.vector.tensor_copy(window[t][:].indirect(offsets[:, a // 16 : b // 16]), probs)
+        def entries(a, b):
+            return offsets[:, a // 16 : b // 16]
 
         nc.gpsimd.memset(far_below[:], -256.0)
         nc.gpsimd.memset(scale_table[0:96, :].bitcast(I32), 0)
         nc.gpsimd.memset(x_planes[:].bitcast(I32), 0)
-        nc.gpsimd.memset(zero[:], 0.0)
 
         nc.sync.dma_start(scale_table[96:P, :].bitcast(I32), x_scales.bitcast(I32).rearrange("o m n -> m o n"))
         nc.sync.dma_start(offsets[:], offs)
@@ -106,36 +104,24 @@ def tile_picked_zvoc_sigmoid_p_kernel(tc, x_words, x_scales, hT, offs, out):
         for o in range(PASSES):
             quantise(0, o)
         nc.vector.tensor_copy(x_codes[0][:], word_table[0][:].indirect(offsets[:]))
-        for c in range(2):
-            nc.vector.tensor_copy(
-                x_codes[1][:, c * HALF : (c + 1) * HALF],
-                word_table[1][:].indirect(offsets[:, c * HALF // 16 : (c + 1) * HALF // 16]),
-            )
+        for a, b in FIRST_CUTS:
+            nc.vector.tensor_copy(x_codes[1][:, a:b], word_table[1][:].indirect(entries(a, b)))
         interleave(nc.scalar.copy, 1, 0)
-        interleave(nc.vector.tensor_copy, 1, 1, 0, SHARE)
-        interleave(nc.scalar.copy, 1, 1, SHARE, P)
+        interleave(nc.vector.tensor_copy, 1, 1)
         quantise(1, 0)
         quantise(1, 1)
 
         probs = [reuse.tile([P, S], F32, name="probs0", offset=0), sbuf("probs1", [P, S], F32)]
-        opening = psum.tile([P, 512], F32, name="opening")
-        product(0, 0, HALF, opening[:, 0:HALF])
-        nc.scalar.activation(probs[0][:, 0:HALF], opening[:, 0:HALF], SIGMOID)
-        scatter(0, 0, HALF, probs[0][:, 0:HALF])
+        for t, cuts in enumerate((FIRST_CUTS, SECOND_CUTS)):
+            banks = [psum.tile([P, 512], F32, name="bank%d%d" % (t, c)) for c in range(len(cuts))]
+            for o in range(PASSES):
+                for (a, b), bank in zip(cuts, banks):
+                    one_pass(t, o, a, b, bank[:, 0 : b - a])
+            for (a, b), bank in zip(cuts, banks):
+                nc.scalar.activation(probs[t][:, a:b], bank[:, 0 : b - a], SIGMOID)
 
-        bank = psum.tile([P, 512], F32, name="bank_a", tag="turn")
-        product(0, HALF, S, bank[:, HALF:S])
-        product(1, 0, P, bank[:, 0:P])
-        nc.scalar.activation(probs[1][:, 0:P], bank[:, 0:P], SIGMOID)
-        nc.vector.tensor_tensor(window[1][:].indirect(offsets[:, 0 : BETWEEN // 16]), probs[1][:, 0:BETWEEN], zero[:], mybir.AluOpType.add)
-
-        nc.scalar.activation(probs[0][:, HALF:S], bank[:, HALF:S], SIGMOID)
-        scatter(0, HALF, S, probs[0][:, HALF:S])
+        nc.vector.tensor_copy(window[0][:].indirect(offsets[:]), probs[0][:])
         nc.sync.dma_start(out[0:P, :], window[0][:])
-
-        bank = psum.tile([P, 512], F32, name="bank_c", tag="opening")
-        product(1, P, HALF, bank[:, P:HALF])
-        product(1, HALF, S, bank[:, HALF:S])
-        nc.scalar.activation(probs[1][:, P:S], bank[:, P:S], SIGMOID)
-        scatter(1, BETWEEN, S, probs[1][:, BETWEEN:S])
+        nc.scalar.activation(window[1][:].indirect(entries(0, HALF)), probs[1][:, 0:HALF], COPY)
+        nc.vector.tensor_copy(window[1][:].indirect(entries(HALF, S)), probs[1][:, HALF:S])
         nc.sync.dma_start(out[P:J, :], window[1][:])

@@ -19,6 +19,7 @@ P = 128
 PACK = 4
 PASSES = K // (P * PACK)
 HALF = S // 2
+OVERLAP = P // 2
 FIRST_CUTS = [(0, 256), (256, 384), (384, 512)]
 SECOND_CUTS = [(0, HALF), (HALF, S)]
 
@@ -51,10 +52,10 @@ def tile_picked_zvoc_sigmoid_p_kernel(tc, x_words, x_scales, hT, offs, out):
             queue = nc.scalar if t == 0 else nc.sync
             queue.dma_start(h_raw[t, o], hT[o * 512 : (o + 1) * 512, t * P : (t + 1) * P].rearrange("(p j) w -> p j w", j=PACK))
 
-        def interleave(copy, t, o):
+        def interleave(copy, t, o, lo=0, hi=P):
             copy(
-                h_grouped[t, o][:].rearrange("p (c i t) -> p c t i", i=4, t=PACK),
-                h_raw[t, o].rearrange("p t (c i) -> p c t i", i=4),
+                h_grouped[t, o][:, lo * PACK : hi * PACK].rearrange("p (c i t) -> p c t i", i=4, t=PACK),
+                h_raw[t, o][:, :, lo:hi].rearrange("p t (c i) -> p c t i", i=4),
             )
 
         def quantise(t, o):
@@ -95,8 +96,10 @@ def tile_picked_zvoc_sigmoid_p_kernel(tc, x_words, x_scales, hT, offs, out):
                 scale_picked[96 + 8 * q : 96 + 8 * q + 8, :].bitcast(I32),
             )
 
+        shared = reuse.tile([P, 3 * S - 2 * OVERLAP], F32, name="shared", offset=0)
         for o in range(PASSES):
-            h_raw[1, o] = reuse.tile([P, PACK, P], F32, name="h_raw1%d" % o, offset=2048 * o)[:]
+            first = o * (2 * S - 2 * OVERLAP)
+            h_raw[1, o] = shared[:, first : first + S].rearrange("p (j w) -> p j w", j=PACK)
             load_h(1, o)
 
         for o in range(PASSES):
@@ -106,12 +109,13 @@ def tile_picked_zvoc_sigmoid_p_kernel(tc, x_words, x_scales, hT, offs, out):
         nc.vector.tensor_copy(x_codes[0][:], word_table[0][:].indirect(offsets[:]))
         for a, b in FIRST_CUTS:
             nc.vector.tensor_copy(x_codes[1][:, a:b], word_table[1][:].indirect(entries(a, b)))
-        interleave(nc.scalar.copy, 1, 0)
+        interleave(nc.scalar.copy, 1, 0, P - OVERLAP, P)
+        interleave(nc.scalar.copy, 1, 0, 0, P - OVERLAP)
         interleave(nc.vector.tensor_copy, 1, 1)
         quantise(1, 0)
         quantise(1, 1)
 
-        probs = [reuse.tile([P, S], F32, name="probs0", offset=0), sbuf("probs1", [P, S], F32)]
+        probs = [shared[:, S - OVERLAP : 2 * S - OVERLAP], sbuf("probs1", [P, S], F32)[:]]
         for t, cuts in enumerate((FIRST_CUTS, SECOND_CUTS)):
             banks = [psum.tile([P, 512], F32, name="bank%d%d" % (t, c)) for c in range(len(cuts))]
             for o in range(PASSES):
@@ -120,7 +124,7 @@ def tile_picked_zvoc_sigmoid_p_kernel(tc, x_words, x_scales, hT, offs, out):
             for (a, b), bank in zip(cuts, banks):
                 nc.scalar.activation(probs[t][:, a:b], bank[:, 0 : b - a], SIGMOID)
 
-        nc.vector.tensor_copy(window[0][:].indirect(offsets[:]), probs[0][:])
+        nc.vector.tensor_copy(window[0][:].indirect(offsets[:]), probs[0])
         nc.sync.dma_start(out[0:P, :], window[0][:])
         nc.scalar.activation(window[1][:].indirect(entries(0, HALF)), probs[1][:, 0:HALF], COPY)
         nc.vector.tensor_copy(window[1][:].indirect(entries(HALF, S)), probs[1][:, HALF:S])

@@ -20,7 +20,8 @@ PACK = 4
 PASSES = K // (P * PACK)
 HALF = S // 2
 OVERLAP = P // 2
-FIRST_CUTS = [(0, 256), (256, 384), (384, 512)]
+FIRST_CUTS = [(0, 128), (128, 384), (384, 512)]
+OPENING = 64
 SECOND_CUTS = [(0, HALF), (HALF, S)]
 
 
@@ -41,12 +42,20 @@ def tile_picked_zvoc_sigmoid_p_kernel(tc, x_words, x_scales, hT, offs, out):
         word_table = [sbuf("word_table%d" % o, [P, T], U32) for o in range(PASSES)]
         x_codes = [sbuf("x_codes%d" % o, [P, S], U32) for o in range(PASSES)]
         window = [sbuf("window%d" % t, [P, T], F32) for t in range(J // P)]
+        zero = sbuf("zero", [P, OPENING], F32)
         far_below = sbuf("far_below", [P, 1], F32)
         h_raw = {(0, o): sbuf("h_raw0%d" % o, [P, PACK, P], F32)[:] for o in range(PASSES)}
         pieces = [(t, o) for t in range(J // P) for o in range(PASSES)]
-        h_grouped = {k: sbuf("h_grouped%d%d" % k, [P, P * PACK], BF16) for k in pieces}
-        h_codes = {k: sbuf("h_codes%d%d" % k, [P, P], U32) for k in pieces}
-        h_planes = {k: sbuf("h_planes%d%d" % k, [P, P], U8) for k in pieces}
+        h_grouped = {k: sbuf("h_grouped%d%d" % k, [P, P * PACK], BF16) for k in pieces if k[0] == 0}
+        h_codes = {(0, o): sbuf("h_codes0%d" % o, [P, P], U32) for o in range(PASSES)}
+        h_planes = {(0, o): sbuf("h_planes0%d" % o, [P, P], U8) for o in range(PASSES)}
+        late_grouped = sbuf("late_grouped", [P, PASSES * P * PACK], BF16)
+        late_codes = sbuf("late_codes", [P, PASSES * P], U32)
+        late_planes = sbuf("late_planes", [P, PASSES * P], U8)
+        for o in range(PASSES):
+            h_grouped[1, o] = late_grouped[:, o * P * PACK : (o + 1) * P * PACK]
+            h_codes[1, o] = late_codes[:, o * P : (o + 1) * P]
+            h_planes[1, o] = late_planes[:, o * P : (o + 1) * P]
 
         def load_h(t, o):
             queue = nc.scalar if t == 0 else nc.sync
@@ -78,6 +87,7 @@ def tile_picked_zvoc_sigmoid_p_kernel(tc, x_words, x_scales, hT, offs, out):
         nc.gpsimd.memset(far_below[:], -256.0)
         nc.gpsimd.memset(scale_table[0:96, :].bitcast(I32), 0)
         nc.gpsimd.memset(x_planes[:].bitcast(I32), 0)
+        nc.gpsimd.memset(zero[:], 0.0)
 
         nc.sync.dma_start(scale_table[96:P, :].bitcast(I32), x_scales.bitcast(I32).rearrange("o m n -> m o n"))
         nc.sync.dma_start(offsets[:], offs)
@@ -124,7 +134,8 @@ def tile_picked_zvoc_sigmoid_p_kernel(tc, x_words, x_scales, hT, offs, out):
             for (a, b), bank in zip(cuts, banks):
                 nc.scalar.activation(probs[t][:, a:b], bank[:, 0 : b - a], SIGMOID)
 
-        nc.vector.tensor_copy(window[0][:].indirect(offsets[:]), probs[0])
+        nc.vector.tensor_tensor(window[0][:].indirect(entries(0, OPENING)), probs[0][:, 0:OPENING], zero[:], mybir.AluOpType.add)
+        nc.vector.tensor_copy(window[0][:].indirect(entries(OPENING, S)), probs[0][:, OPENING:S])
         nc.sync.dma_start(out[0:P, :], window[0][:])
         nc.scalar.activation(window[1][:].indirect(entries(0, HALF)), probs[1][:, 0:HALF], COPY)
         nc.vector.tensor_copy(window[1][:].indirect(entries(HALF, S)), probs[1][:, HALF:S])

@@ -19,10 +19,10 @@ P = 128
 PACK = 4
 PASSES = K // (P * PACK)
 HALF = S // 2
-OVERLAP = P // 2
-FIRST_CUTS = [(0, 128), (128, 384), (384, 512)]
-OPENING = 64
+OPENING = P
+FIRST_CUTS = [(0, OPENING), (OPENING, OPENING + HALF), (OPENING + HALF, S)]
 SECOND_CUTS = [(0, HALF), (HALF, S)]
+OVERLAP = P // 2
 
 
 def tile_picked_zvoc_sigmoid_p_kernel(tc, x_words, x_scales, hT, offs, out):
@@ -70,15 +70,15 @@ def tile_picked_zvoc_sigmoid_p_kernel(tc, x_words, x_scales, hT, offs, out):
         def quantise(t, o):
             nc.vector.quantize_mx(out=h_codes[t, o][:].bitcast(FP8X4), scales=h_planes[t, o][:], in_=h_grouped[t, o][:])
 
-        def one_pass(t, o, a, b, logits):
+        def one_pass(t, o, a, b, logits, first):
             nc.tensor.matmul_mx(
                 out=logits,
                 lhsT=h_codes[t, o][:].bitcast(FP8X4),
                 lhsT_scale=h_planes[t, o][:],
                 rhs=x_codes[o][:, a:b].bitcast(FP8X4),
                 rhs_scale=x_planes[:, o * S + a : o * S + b],
-                start=(o == 0),
-                stop=(o == PASSES - 1),
+                start=first,
+                stop=not first,
             )
 
         def entries(a, b):
@@ -119,24 +119,34 @@ def tile_picked_zvoc_sigmoid_p_kernel(tc, x_words, x_scales, hT, offs, out):
         nc.vector.tensor_copy(x_codes[0][:], word_table[0][:].indirect(offsets[:]))
         for a, b in FIRST_CUTS:
             nc.vector.tensor_copy(x_codes[1][:, a:b], word_table[1][:].indirect(entries(a, b)))
-        interleave(nc.scalar.copy, 1, 0, P - OVERLAP, P)
-        interleave(nc.scalar.copy, 1, 0, 0, P - OVERLAP)
-        interleave(nc.vector.tensor_copy, 1, 1)
-        quantise(1, 0)
-        quantise(1, 1)
 
         probs = [shared[:, S - OVERLAP : 2 * S - OVERLAP], sbuf("probs1", [P, S], F32)[:]]
-        for t, cuts in enumerate((FIRST_CUTS, SECOND_CUTS)):
-            banks = [psum.tile([P, 512], F32, name="bank%d%d" % (t, c)) for c in range(len(cuts))]
+        opening_bank = psum.tile([P, 512], F32, name="opening_bank")
+        rest_bank = psum.tile([P, 512], F32, name="rest_bank")
+        for o in (0, 1):
+            one_pass(0, o, 0, OPENING, opening_bank[:, 0:OPENING], o == 0)
+        interleave(nc.scalar.copy, 1, 0, P - OVERLAP, P)
+        interleave(nc.scalar.copy, 1, 0, 0, P - OVERLAP)
+        nc.scalar.activation(probs[0][:, 0:OPENING], opening_bank[:, 0:OPENING], SIGMOID)
+        for a, b in FIRST_CUTS[1:]:
             for o in range(PASSES):
-                for (a, b), bank in zip(cuts, banks):
-                    one_pass(t, o, a, b, bank[:, 0 : b - a])
-            for (a, b), bank in zip(cuts, banks):
-                nc.scalar.activation(probs[t][:, a:b], bank[:, 0 : b - a], SIGMOID)
-
+                one_pass(0, o, a, b, rest_bank[:, a:b], o == 0)
+        quantise(1, 0)
         nc.vector.tensor_tensor(window[0][:].indirect(entries(0, OPENING)), probs[0][:, 0:OPENING], zero[:], mybir.AluOpType.add)
+
+        interleave(nc.scalar.copy, 1, 1, 0, OVERLAP)
+        interleave(nc.scalar.copy, 1, 1, OVERLAP, P)
+        quantise(1, 1)
+        nc.scalar.activation(probs[0][:, OPENING:S], rest_bank[:, OPENING:S], SIGMOID)
         nc.vector.tensor_copy(window[0][:].indirect(entries(OPENING, S)), probs[0][:, OPENING:S])
         nc.sync.dma_start(out[0:P, :], window[0][:])
+
+        banks = [psum.tile([P, 512], F32, name="bank1%d" % c) for c in range(len(SECOND_CUTS))]
+        for o in range(PASSES):
+            for (a, b), bank in zip(SECOND_CUTS, banks):
+                one_pass(1, o, a, b, bank[:, 0 : b - a], o == 0)
+        for (a, b), bank in zip(SECOND_CUTS, banks):
+            nc.scalar.activation(probs[1][:, a:b], bank[:, 0 : b - a], SIGMOID)
         nc.scalar.activation(window[1][:].indirect(entries(0, HALF)), probs[1][:, 0:HALF], COPY)
         nc.vector.tensor_copy(window[1][:].indirect(entries(HALF, S)), probs[1][:, HALF:S])
         nc.sync.dma_start(out[P:J, :], window[1][:])

@@ -19,10 +19,11 @@ P = 128
 PACK = 4
 PASSES = K // (P * PACK)
 HALF = S // 2
-OPENING = P
-FIRST_CUTS = [(0, OPENING), (OPENING, OPENING + HALF), (OPENING + HALF, S)]
+OPENING = 96
+FIRST_CUTS = [(0, P), (P, P + HALF), (P + HALF, S)]
 SECOND_CUTS = [(0, HALF), (HALF, S)]
 OVERLAP = P // 2
+SCALAR_SHARE = 96
 
 
 def tile_picked_zvoc_sigmoid_p_kernel(tc, x_words, x_scales, hT, offs, out):
@@ -70,7 +71,7 @@ def tile_picked_zvoc_sigmoid_p_kernel(tc, x_words, x_scales, hT, offs, out):
         def quantise(t, o):
             nc.vector.quantize_mx(out=h_codes[t, o][:].bitcast(FP8X4), scales=h_planes[t, o][:], in_=h_grouped[t, o][:])
 
-        def one_pass(t, o, a, b, logits, first):
+        def one_pass(t, o, a, b, logits, first, last):
             nc.tensor.matmul_mx(
                 out=logits,
                 lhsT=h_codes[t, o][:].bitcast(FP8X4),
@@ -78,7 +79,7 @@ def tile_picked_zvoc_sigmoid_p_kernel(tc, x_words, x_scales, hT, offs, out):
                 rhs=x_codes[o][:, a:b].bitcast(FP8X4),
                 rhs_scale=x_planes[:, o * S + a : o * S + b],
                 start=first,
-                stop=not first,
+                stop=last,
             )
 
         def entries(a, b):
@@ -106,10 +107,11 @@ def tile_picked_zvoc_sigmoid_p_kernel(tc, x_words, x_scales, hT, offs, out):
                 scale_picked[96 + 8 * q : 96 + 8 * q + 8, :].bitcast(I32),
             )
 
-        shared = reuse.tile([P, 3 * S - 2 * OVERLAP], F32, name="shared", offset=0)
+        lead = SCALAR_SHARE // 2
+        starts = [0, S - OVERLAP + P + HALF - lead]
+        shared = reuse.tile([P, starts[1] + S], F32, name="shared", offset=0)
         for o in range(PASSES):
-            first = o * (2 * S - 2 * OVERLAP)
-            h_raw[1, o] = shared[:, first : first + S].rearrange("p (j w) -> p j w", j=PACK)
+            h_raw[1, o] = shared[:, starts[o] : starts[o] + S].rearrange("p (j w) -> p j w", j=PACK)
             load_h(1, o)
 
         for o in range(PASSES):
@@ -121,30 +123,37 @@ def tile_picked_zvoc_sigmoid_p_kernel(tc, x_words, x_scales, hT, offs, out):
             nc.vector.tensor_copy(x_codes[1][:, a:b], word_table[1][:].indirect(entries(a, b)))
 
         probs = [shared[:, S - OVERLAP : 2 * S - OVERLAP], sbuf("probs1", [P, S], F32)[:]]
-        opening_bank = psum.tile([P, 512], F32, name="opening_bank")
-        rest_bank = psum.tile([P, 512], F32, name="rest_bank")
-        for o in (0, 1):
-            one_pass(0, o, 0, OPENING, opening_bank[:, 0:OPENING], o == 0)
+        first_banks = [psum.tile([P, 512], F32, name="bank0%d" % c) for c in range(len(FIRST_CUTS))]
+
+        def first_pass(c, o):
+            a, b = FIRST_CUTS[c]
+            one_pass(0, o, a, b, first_banks[c][:, 0 : b - a], o == 0, o == 1)
+
+        def first_sigmoid(c):
+            a, b = FIRST_CUTS[c]
+            nc.scalar.activation(probs[0][:, a:b], first_banks[c][:, 0 : b - a], SIGMOID)
+
+        for c, o in ((0, 0), (0, 1), (2, 0), (1, 0), (1, 1), (2, 1)):
+            first_pass(c, o)
         interleave(nc.scalar.copy, 1, 0, P - OVERLAP, P)
         interleave(nc.scalar.copy, 1, 0, 0, P - OVERLAP)
-        nc.scalar.activation(probs[0][:, 0:OPENING], opening_bank[:, 0:OPENING], SIGMOID)
-        for a, b in FIRST_CUTS[1:]:
-            for o in range(PASSES):
-                one_pass(0, o, a, b, rest_bank[:, a:b], o == 0)
+        first_sigmoid(0)
+        interleave(nc.vector.tensor_copy, 1, 1, SCALAR_SHARE, P)
         quantise(1, 0)
         nc.vector.tensor_tensor(window[0][:].indirect(entries(0, OPENING)), probs[0][:, 0:OPENING], zero[:], mybir.AluOpType.add)
 
-        interleave(nc.scalar.copy, 1, 1, 0, OVERLAP)
-        interleave(nc.scalar.copy, 1, 1, OVERLAP, P)
+        interleave(nc.scalar.copy, 1, 1, 0, lead)
+        interleave(nc.scalar.copy, 1, 1, lead, SCALAR_SHARE)
         quantise(1, 1)
-        nc.scalar.activation(probs[0][:, OPENING:S], rest_bank[:, OPENING:S], SIGMOID)
+        first_sigmoid(1)
+        first_sigmoid(2)
         nc.vector.tensor_copy(window[0][:].indirect(entries(OPENING, S)), probs[0][:, OPENING:S])
         nc.sync.dma_start(out[0:P, :], window[0][:])
 
         banks = [psum.tile([P, 512], F32, name="bank1%d" % c) for c in range(len(SECOND_CUTS))]
         for o in range(PASSES):
             for (a, b), bank in zip(SECOND_CUTS, banks):
-                one_pass(1, o, a, b, bank[:, 0 : b - a], o == 0)
+                one_pass(1, o, a, b, bank[:, 0 : b - a], o == 0, o == 1)
         for (a, b), bank in zip(SECOND_CUTS, banks):
             nc.scalar.activation(probs[1][:, a:b], bank[:, 0 : b - a], SIGMOID)
         nc.scalar.activation(window[1][:].indirect(entries(0, HALF)), probs[1][:, 0:HALF], COPY)

@@ -22,8 +22,8 @@ HALF = S // 2
 OPENING = 96
 FIRST_CUTS = [(0, P), (P, P + HALF), (P + HALF, S)]
 SECOND_CUTS = [(0, HALF), (HALF, S)]
-OVERLAP = P // 2
-SCALAR_SHARE = 96
+GPSIMD_SHARE = 32
+OVERLAP = 32
 
 
 def tile_picked_zvoc_sigmoid_p_kernel(tc, x_words, x_scales, hT, offs, out):
@@ -68,6 +68,9 @@ def tile_picked_zvoc_sigmoid_p_kernel(tc, x_words, x_scales, hT, offs, out):
                 h_raw[t, o][:, :, lo:hi].rearrange("p t (c i) -> p c t i", i=4),
             )
 
+        def gpsimd_round(dst, src):
+            nc.gpsimd.tensor_scalar(dst, src, 1.0, 0.0, mybir.AluOpType.mult, mybir.AluOpType.add)
+
         def quantise(t, o):
             nc.vector.quantize_mx(out=h_codes[t, o][:].bitcast(FP8X4), scales=h_planes[t, o][:], in_=h_grouped[t, o][:])
 
@@ -107,7 +110,7 @@ def tile_picked_zvoc_sigmoid_p_kernel(tc, x_words, x_scales, hT, offs, out):
                 scale_picked[96 + 8 * q : 96 + 8 * q + 8, :].bitcast(I32),
             )
 
-        lead = SCALAR_SHARE // 2
+        lead = P // 2
         starts = [0, S - OVERLAP + P + HALF - lead]
         shared = reuse.tile([P, starts[1] + S], F32, name="shared", offset=0)
         for o in range(PASSES):
@@ -135,15 +138,15 @@ def tile_picked_zvoc_sigmoid_p_kernel(tc, x_words, x_scales, hT, offs, out):
 
         for c, o in ((0, 0), (0, 1), (2, 0), (1, 0), (1, 1), (2, 1)):
             first_pass(c, o)
+        interleave(gpsimd_round, 1, 0, 0, GPSIMD_SHARE)
         interleave(nc.scalar.copy, 1, 0, P - OVERLAP, P)
-        interleave(nc.scalar.copy, 1, 0, 0, P - OVERLAP)
+        interleave(nc.scalar.copy, 1, 0, GPSIMD_SHARE, P - OVERLAP)
         first_sigmoid(0)
-        interleave(nc.vector.tensor_copy, 1, 1, SCALAR_SHARE, P)
         quantise(1, 0)
         nc.vector.tensor_tensor(window[0][:].indirect(entries(0, OPENING)), probs[0][:, 0:OPENING], zero[:], mybir.AluOpType.add)
 
         interleave(nc.scalar.copy, 1, 1, 0, lead)
-        interleave(nc.scalar.copy, 1, 1, lead, SCALAR_SHARE)
+        interleave(nc.scalar.copy, 1, 1, lead, P)
         quantise(1, 1)
         first_sigmoid(1)
         first_sigmoid(2)

@@ -22,7 +22,7 @@ HALF = S // 2
 OPENING = 96
 FIRST_CUTS = [(0, P), (P, P + HALF), (P + HALF, S)]
 SECOND_CUTS = [(0, HALF), (HALF, S)]
-GPSIMD_SHARE = 32
+GPSIMD_SHARE = 48
 OVERLAP = 32
 
 

from contextlib import ExitStack

import concourse.mybir as mybir

K, T, S, J = 1024, 2048, 512, 256
FLOPS = 2 * K * S * J

F32 = mybir.dt.float32
BF16 = mybir.dt.bfloat16
I32 = mybir.dt.int32
U32 = mybir.dt.uint32
U16 = mybir.dt.uint16
U8 = mybir.dt.uint8
FP8X4 = mybir.dt.float8_e4m3fn_x4
SIGMOID = mybir.ActivationFunctionType.Sigmoid
COPY = mybir.ActivationFunctionType.Copy

P = 128
PACK = 4
PASSES = K // (P * PACK)
HALF = S // 2
OPENING = 96
FIRST_CUTS = [(0, P), (P, P + HALF), (P + HALF, S)]
SECOND_CUTS = [(0, HALF), (HALF, S)]
GPSIMD_SHARE = 48
OVERLAP = 32


def tile_picked_zvoc_sigmoid_p_kernel(tc, x_words, x_scales, hT, offs, out):
    nc = tc.nc
    with ExitStack() as ctx:
        keep = ctx.enter_context(tc.tile_pool(name="keep", bufs=1))
        reuse = ctx.enter_context(tc.tile_pool(name="reuse", bufs=1))
        psum = ctx.enter_context(tc.psum_pool(name="psum", bufs=1))

        def sbuf(name, shape, dtype):
            return keep.tile(shape, dtype, name=name, align_bytes=64)

        offsets = keep.tile([P, S // 16], U16, name="offsets")
        scale_table = reuse.tile([P, T], U8, name="scale_table", offset=1024)
        scale_picked = sbuf("scale_picked", [P, S], U8)
        x_planes = sbuf("x_planes", [P, PASSES * S], U8)
        word_table = [sbuf("word_table%d" % o, [P, T], U32) for o in range(PASSES)]
        x_codes = [sbuf("x_codes%d" % o, [P, S], U32) for o in range(PASSES)]
        window = [sbuf("window%d" % t, [P, T], F32) for t in range(J // P)]
        zero = sbuf("zero", [P, OPENING], F32)
        far_below = sbuf("far_below", [P, 1], F32)
        h_raw = {(0, o): sbuf("h_raw0%d" % o, [P, PACK, P], F32)[:] for o in range(PASSES)}
        pieces = [(t, o) for t in range(J // P) for o in range(PASSES)]
        h_grouped = {k: sbuf("h_grouped%d%d" % k, [P, P * PACK], BF16) for k in pieces if k[0] == 0}
        h_codes = {(0, o): sbuf("h_codes0%d" % o, [P, P], U32) for o in range(PASSES)}
        h_planes = {(0, o): sbuf("h_planes0%d" % o, [P, P], U8) for o in range(PASSES)}
        late_grouped = sbuf("late_grouped", [P, PASSES * P * PACK], BF16)
        late_codes = sbuf("late_codes", [P, PASSES * P], U32)
        late_planes = sbuf("late_planes", [P, PASSES * P], U8)
        for o in range(PASSES):
            h_grouped[1, o] = late_grouped[:, o * P * PACK : (o + 1) * P * PACK]
            h_codes[1, o] = late_codes[:, o * P : (o + 1) * P]
            h_planes[1, o] = late_planes[:, o * P : (o + 1) * P]

        def load_h(t, o):
            queue = nc.scalar if t == 0 else nc.sync
            queue.dma_start(h_raw[t, o], hT[o * 512 : (o + 1) * 512, t * P : (t + 1) * P].rearrange("(p j) w -> p j w", j=PACK))

        def interleave(copy, t, o, lo=0, hi=P):
            copy(
                h_grouped[t, o][:, lo * PACK : hi * PACK].rearrange("p (c i t) -> p c t i", i=4, t=PACK),
                h_raw[t, o][:, :, lo:hi].rearrange("p t (c i) -> p c t i", i=4),
            )

        def gpsimd_round(dst, src):
            nc.gpsimd.tensor_scalar(dst, src, 1.0, 0.0, mybir.AluOpType.mult, mybir.AluOpType.add)

        def quantise(t, o):
            nc.vector.quantize_mx(out=h_codes[t, o][:].bitcast(FP8X4), scales=h_planes[t, o][:], in_=h_grouped[t, o][:])

        def one_pass(t, o, a, b, logits, first, last):
            nc.tensor.matmul_mx(
                out=logits,
                lhsT=h_codes[t, o][:].bitcast(FP8X4),
                lhsT_scale=h_planes[t, o][:],
                rhs=x_codes[o][:, a:b].bitcast(FP8X4),
                rhs_scale=x_planes[:, o * S + a : o * S + b],
                start=first,
                stop=last,
            )

        def entries(a, b):
            return offsets[:, a // 16 : b // 16]

        nc.gpsimd.memset(far_below[:], -256.0)
        nc.gpsimd.memset(scale_table[0:96, :].bitcast(I32), 0)
        nc.gpsimd.memset(x_planes[:].bitcast(I32), 0)
        nc.gpsimd.memset(zero[:], 0.0)

        nc.sync.dma_start(scale_table[96:P, :].bitcast(I32), x_scales.bitcast(I32).rearrange("o m n -> m o n"))
        nc.sync.dma_start(offsets[:], offs)
        load_h(0, 0)
        load_h(0, 1)
        for o in range(PASSES):
            nc.sync.dma_start(word_table[o][:].bitcast(I32), x_words[o].rearrange("p n t -> p (n t)").bitcast(I32))

        nc.vector.memset(window[0][:].bitcast(I32), 0)
        nc.scalar.activation(window[1][:], far_below[:, 0:1].to_broadcast([P, T]), SIGMOID)

        nc.vector.tensor_copy(scale_picked[:], scale_table[:].indirect(offsets[:]))
        for q in (0, 2, 1, 3):
            nc.sync.dma_start(
                x_planes[32 * q : 32 * q + 4, :].bitcast(I32).rearrange("p (o n) -> p o n", o=PASSES),
                scale_picked[96 + 8 * q : 96 + 8 * q + 8, :].bitcast(I32),
            )

        lead = P // 2
        starts = [0, S - OVERLAP + P + HALF - lead]
        shared = reuse.tile([P, starts[1] + S], F32, name="shared", offset=0)
        for o in range(PASSES):
            h_raw[1, o] = shared[:, starts[o] : starts[o] + S].rearrange("p (j w) -> p j w", j=PACK)
            load_h(1, o)

        for o in range(PASSES):
            interleave(nc.vector.tensor_copy, 0, o)
        for o in range(PASSES):
            quantise(0, o)
        nc.vector.tensor_copy(x_codes[0][:], word_table[0][:].indirect(offsets[:]))
        for a, b in FIRST_CUTS:
            nc.vector.tensor_copy(x_codes[1][:, a:b], word_table[1][:].indirect(entries(a, b)))

        probs = [shared[:, S - OVERLAP : 2 * S - OVERLAP], sbuf("probs1", [P, S], F32)[:]]
        first_banks = [psum.tile([P, 512], F32, name="bank0%d" % c) for c in range(len(FIRST_CUTS))]

        def first_pass(c, o):
            a, b = FIRST_CUTS[c]
            one_pass(0, o, a, b, first_banks[c][:, 0 : b - a], o == 0, o == 1)

        def first_sigmoid(c):
            a, b = FIRST_CUTS[c]
            nc.scalar.activation(probs[0][:, a:b], first_banks[c][:, 0 : b - a], SIGMOID)

        for c, o in ((0, 0), (0, 1), (2, 0), (1, 0), (1, 1), (2, 1)):
            first_pass(c, o)
        interleave(gpsimd_round, 1, 0, 0, GPSIMD_SHARE)
        interleave(nc.scalar.copy, 1, 0, P - OVERLAP, P)
        interleave(nc.scalar.copy, 1, 0, GPSIMD_SHARE, P - OVERLAP)
        first_sigmoid(0)
        quantise(1, 0)
        nc.vector.tensor_tensor(window[0][:].indirect(entries(0, OPENING)), probs[0][:, 0:OPENING], zero[:], mybir.AluOpType.add)

        interleave(nc.scalar.copy, 1, 1, 0, lead)
        interleave(nc.scalar.copy, 1, 1, lead, P)
        quantise(1, 1)
        first_sigmoid(1)
        first_sigmoid(2)
        nc.vector.tensor_copy(window[0][:].indirect(entries(OPENING, S)), probs[0][:, OPENING:S])
        nc.sync.dma_start(out[0:P, :], window[0][:])

        banks = [psum.tile([P, 512], F32, name="bank1%d" % c) for c in range(len(SECOND_CUTS))]
        for o in range(PASSES):
            for (a, b), bank in zip(SECOND_CUTS, banks):
                one_pass(1, o, a, b, bank[:, 0 : b - a], o == 0, o == 1)
        for (a, b), bank in zip(SECOND_CUTS, banks):
            nc.scalar.activation(probs[1][:, a:b], bank[:, 0 : b - a], SIGMOID)
        nc.scalar.activation(window[1][:].indirect(entries(0, HALF)), probs[1][:, 0:HALF], COPY)
        nc.vector.tensor_copy(window[1][:].indirect(entries(HALF, S)), probs[1][:, HALF:S])
        nc.sync.dma_start(out[P:J, :], window[1][:])
